import numpy as np
import ml_dtypes


def mxq(x, axis, fmt="e4m3"):
    dtype, down = {"e4m3": (ml_dtypes.float8_e4m3fn, 7), "e5m2": (ml_dtypes.float8_e5m2, 14)}[fmt]
    v = np.moveaxis(np.asarray(x, np.float32).astype(ml_dtypes.bfloat16).astype(np.float64), axis, -1)
    blocks = v.reshape(v.shape[:-1] + (-1, 32))
    amax = np.abs(blocks).max(-1, keepdims=True)
    byte = np.maximum(np.where(amax > 0, np.frexp(amax)[1] - 1 + 127, 0) - down, 1)
    scale = np.exp2(byte - 127.0)
    codes = (blocks / scale).astype(np.float32).astype(dtype).astype(np.float64)
    return np.moveaxis((codes * scale).reshape(v.shape), -1, axis)


WIDE = False


def mx_kscale(k):
    if not WIDE:
        return np.ones(k)
    levels = np.array([10, -10, 5, -5, 0])
    if k % 512:
        return np.exp2(np.random.permutation(np.resize(levels, k // 32))).repeat(32)
    a = np.empty((k // 512, 16))
    for p in range(k // 512):
        a[p, :8] = np.random.permutation(np.resize(levels, 8))
        for g in range(8):
            far = levels[np.abs(levels - a[p, g]) >= 10]
            a[p, g + 8] = far[np.random.randint(len(far))]
    return np.exp2(a.ravel()).repeat(32)


def f64(x):
    return np.asarray(x).astype(np.float64)


E2M1 = np.array([0.0, 0.5, 1.0, 1.5, 2.0, 3.0, 4.0, 6.0, -0.0, -0.5, -1.0, -1.5, -2.0, -3.0, -4.0, -6.0])


def pack_weight(w, fmt):
    k, n = w.shape
    w = f64(np.asarray(w, np.float32).astype(ml_dtypes.bfloat16)).reshape(k // 32, 32, n)
    amax = np.abs(w).max(1)
    if fmt == "e4m3":
        byte = np.frexp(amax)[1] - 1 + 127 - 7
    else:
        mant, ex = np.frexp(amax / 6.0)
        byte = np.where(mant > 0.5, ex, ex - 1) + 127
    byte = np.clip(np.where(amax > 0, byte, 1), 1, 254)
    scaled = (w * np.exp2(127.0 - byte)[:, None, :]).reshape(k, n).astype(np.float32)
    by_word = np.ascontiguousarray(scaled.reshape(k // 512, 128, 4, n).transpose(0, 1, 3, 2))
    if fmt == "e4m3":
        words = by_word.astype(ml_dtypes.float8_e4m3fn).view(np.uint8)
    else:
        c = by_word.astype(ml_dtypes.float4_e2m1fn).view(np.uint8) & 0xF
        words = (c[..., 0::2] | (c[..., 1::2] << 4)).reshape(k // 512, 128, 2 * n)
    return np.ascontiguousarray(words), np.ascontiguousarray(byte.astype(np.uint8).reshape(k // 512, 16, n))


def unpack_weight(words, scales, fmt):
    g, _, n = scales.shape
    words = np.ascontiguousarray(words).reshape(g, 128, n, -1)
    if fmt == "e4m3":
        vals = words.view(ml_dtypes.float8_e4m3fn).astype(np.float64)
    else:
        nib = np.empty((g, 128, n, 4), np.uint8)
        nib[..., 0::2] = words & 0xF
        nib[..., 1::2] = words >> 4
        vals = E2M1[nib]
    vals = vals * np.repeat(np.exp2(scales.astype(np.float64) - 127.0), 8, axis=1)[..., None]
    return vals.transpose(0, 1, 3, 2).reshape(g * 512, n)


def bf(x):
    return np.asarray(x, np.float32).astype(ml_dtypes.bfloat16)


def planes(Y):
    r, m = Y.shape
    b = f64(bf(Y)).reshape(r // 32, 32, m)
    amax = np.abs(b).max(1)
    byte = np.clip(np.where(amax > 0, np.frexp(amax)[1] - 1 + 127 - 7, 1), 1, 254)
    codes = (b * np.exp2(127.0 - byte)[:, None, :]).reshape(r, m).astype(np.float32).astype(ml_dtypes.float8_e4m3fn).view(np.uint8)
    words = codes.reshape(r // 512, 128, 4, m).transpose(0, 1, 3, 2)
    return np.ascontiguousarray(words), np.ascontiguousarray(byte.astype(np.uint8).reshape(r // 512, 16, m))


K, L, T, N = 512, 1024, 512, 512


def setup_inputs():
    n = np.random.standard_normal
    fk = mx_kscale(K)
    fl = mx_kscale(L)
    wap = pack_weight(n((K, N)) * 1 / np.sqrt(K) * fk[:, None], "e2m1")
    xqp = pack_weight(n((L, T)) / fl[:, None], "e4m3")
    wqp = pack_weight(n((L, N)) * 1 / np.sqrt(L) * fl[:, None], "e2m1")
    wsp = pack_weight(n((L, N)) * 1 / np.sqrt(L) * fl[:, None], "e4m3")
    return {
        "xt": (n((K, T)) / fk[:, None]).astype(np.float32),
        "wa_words": wap[0],
        "wa_scales": wap[1],
        "xq_words": xqp[0],
        "xq_scales": xqp[1],
        "wq_words": wqp[0],
        "wq_scales": wqp[1],
        "wb": (n((K, N)) * 1 / np.sqrt(K) * fk[:, None]).astype(np.float32),
        "ws_words": wsp[0],
        "ws_scales": wsp[1],
    }


def reference(xt, wa_words, wa_scales, xq_words, xq_scales, wq_words, wq_scales, wb, ws_words, ws_scales):
    wau = unpack_weight(wa_words, wa_scales, "e2m1")
    xqu = unpack_weight(xq_words, xq_scales, "e4m3")
    wqu = unpack_weight(wq_words, wq_scales, "e2m1")
    wsu = unpack_weight(ws_words, ws_scales, "e4m3")
    xtq = mxq(f64(xt), 0, "e4m3")
    p = wau.T @ xtq + wqu.T @ xqu
    wbq = mxq(f64(wb), 0, "e4m3")
    r = wbq.T @ xtq + wsu.T @ xqu
    y = p * r / (1.0 + np.abs(r))
    words, scales = planes(y)
    return y, words, scales

@@ -1,0 +1,370 @@
+from contextlib import ExitStack
+
+import concourse.mybir as mybir
+from concourse.masks import make_identity
+
+K, L, T, N = 512, 1024, 512, 512
+FLOPS = 2 * 2 * (K + L) * T * N
+
+F32 = mybir.dt.float32
+BF16 = mybir.dt.bfloat16
+I32 = mybir.dt.int32
+U32 = mybir.dt.uint32
+U8 = mybir.dt.uint8
+FP8X4 = mybir.dt.float8_e4m3fn_x4
+FP4X4 = mybir.dt.float4_e2m1fn_x4
+ACT = mybir.ActivationFunctionType
+MULT = mybir.AluOpType.mult
+
+P = 128
+PACK = 4
+TILES = T // P
+HALF = N // 2
+QUADS = 4
+S_COLS = 80
+
+
+def tile_mix_product_of_two_sums_pl_kernel(
+    tc, xt, wa_words, wa_scales, xq_words, xq_scales, wq_words, wq_scales, wb, ws_words, ws_scales,
+    out_0, out_1, out_2,
+):
+    nc = tc.nc
+    with ExitStack() as ctx:
+        sb = ctx.enter_context(tc.tile_pool(name="sb", bufs=1))
+        ps = ctx.enter_context(tc.psum_pool(name="ps", bufs=1))
+        ctx.enter_context(tc.manual_schedule())
+
+        def new(name, shape, dtype):
+            return sb.tile(shape, dtype, name=name, align_bytes=64)
+
+        xt_rows = xt.rearrange("(p j) t -> p j t", j=PACK)
+        wb_rows = wb.rearrange("(p j) n -> p j n", j=PACK)
+        out_rows = out_0.rearrange("(p j) t -> p j t", j=PACK)
+        xq_src = xq_words.rearrange("z p t r -> p z (t r)").bitcast(I32)
+        ws_src = ws_words.rearrange("z p n r -> p z (n r)").bitcast(I32)
+
+        xt_raw = [new("xt_raw%d" % c, [P, PACK, P], F32) for c in range(TILES)]
+        xt_bf = [new("xt_bf%d" % c, [P, P, PACK], BF16) for c in range(TILES)]
+        xt_codes = [new("xt_codes%d" % c, [P, P], U32) for c in range(TILES)]
+        xt_plane = [new("xt_plane%d" % c, [P, P], U8) for c in range(TILES)]
+        wb_raw = [new("wb_raw%d" % h, [P, PACK, HALF], F32) for h in range(2)]
+        wb_bf = [new("wb_bf%d" % h, [P, HALF, PACK], BF16) for h in range(2)]
+        wb_codes = [new("wb_codes%d" % h, [P, HALF], U32) for h in range(2)]
+        wb_plane = [new("wb_plane%d" % h, [P, HALF], U8) for h in range(2)]
+        xq_codes = [new("xq_codes%d" % h, [P, 2, 2 * P], I32) for h in range(2)]
+        ws_codes = [new("ws_codes%d" % h, [P, 2, HALF], I32) for h in range(2)]
+        wa_codes = new("wa_codes", [P, 2 * N], U8)
+        wq_codes = new("wq_codes", [P, 2, 2 * N], U8)
+        early = new("early", [P, 2, N], U8)
+        late = new("late", [P, 3, N], U8)
+        ident = new("ident", [P, P], F32)
+        warm = new("warm", [P, 16], F32)
+        warm_out = new("warm_out", [P, 16], F32)
+        y_codes = new("y_codes", [P, T], U32)
+        y_plane = new("y_plane", [P, T], U8)
+        y_tok = [new("y_tok%d" % c, [P, PACK, P], F32) for c in range(TILES)]
+        y_out = [new("y_out%d" % c, [P, PACK, P], F32) for c in range(TILES)]
+        y_bf = [new("y_bf%d" % c, [P, P, PACK], BF16) for c in range(TILES)]
+        units = [(c, h) for h in range(2) for c in range(TILES)]
+        mag = {u: new("mag%d_%d" % u, [P, PACK, HALF // PACK], F32) for u in units}
+        root = {u: new("root%d_%d" % u, [P, PACK, HALF // PACK], F32) for u in units}
+        inv = {u: new("inv%d_%d" % u, [P, PACK, HALF // PACK], F32) for u in units}
+        soft = {u: new("soft%d_%d" % u, [P, PACK, HALF // PACK], F32) for u in units}
+        r_ps = {}
+        R_TAG = {(0, 0): "a", (1, 0): "b", (0, 1): "c", (1, 1): "d", (2, 0): "a", (3, 0): "b"}
+        Y_TAG = ["c", "d", "p_ps0", "p_ps1"]
+
+        def r_bank(c, h):
+            if c >= 2:
+                h = 0
+            if (c, h) not in r_ps:
+                r_ps[c, h] = ps.tile([P, N], F32, name="r_ps%d_%d" % (c, h), tag=R_TAG[c, h])
+            return r_ps[c, h]
+
+        p_ps = [ps.tile([P, N], F32, name="p_ps%d" % c) for c in range(TILES)]
+
+        def tok(c):
+            return slice(c * P, (c + 1) * P)
+
+        def half(h):
+            return slice(h * HALF, (h + 1) * HALF)
+
+        def dealt(bank, h):
+            return bank[:, half(h)].rearrange("t (m j) -> t j m", j=PACK)
+
+        def load_xt(c):
+            nc.sync.dma_start(out=xt_raw[c][:], in_=xt_rows[:, :, tok(c)])
+
+        def load_wb(h):
+            nc.sync.dma_start(out=wb_raw[h][:], in_=wb_rows[:, :, half(h)])
+
+        def load_xq(h):
+            nc.sync.dma_start(out=xq_codes[h][:], in_=xq_src[:, :, half(h)])
+
+        def load_ws(h):
+            nc.sync.dma_start(out=ws_codes[h][:], in_=ws_src[:, :, half(h)])
+
+        def load_wa():
+            nc.sync.dma_start(out=wa_codes[:].bitcast(I32), in_=wa_words[0].bitcast(I32))
+
+        def load_wq():
+            nc.sync.dma_start(out=wq_codes[:].bitcast(I32), in_=wq_words.rearrange("z p b -> p z b").bitcast(I32))
+
+        def load_plane(eng, dst, src):
+            for q in range(QUADS):
+                eng.dma_start(
+                    out=dst[32 * q : 32 * q + 4].bitcast(I32),
+                    in_=src[:, 4 * q : 4 * q + 4, :].rearrange("z r c -> r z c").bitcast(I32),
+                )
+
+        def load_ws_plane(eng):
+            for q in range(QUADS):
+                eng.dma_start(
+                    out=early[32 * q + 4 : 32 * q + 12, 0, :].bitcast(I32),
+                    in_=ws_scales[:, 4 * q : 4 * q + 4, :].bitcast(I32),
+                )
+
+        def group(copy, dst, src, lo, hi):
+            copy(
+                out=dst[:, lo:hi, :].rearrange("p (c i) j -> p c j i", i=4),
+                in_=src[:, :, lo:hi].rearrange("p j (c i) -> p c j i", i=4),
+            )
+
+        def quant(codes, plane, src):
+            nc.vector.quantize_mx(out=codes.bitcast(FP8X4), scales=plane, in_=src[:].rearrange("p c j -> p (c j)"))
+
+        def copier(e):
+            return {"DVE": nc.vector.tensor_copy, "ACT": nc.scalar.copy, "POOL": nc.gpsimd.tensor_copy}[e]
+
+        def group_xt(c, e="DVE"):
+            group(copier(e), xt_bf[c], xt_raw[c], 0, P)
+
+        def quant_xt(c):
+            quant(xt_codes[c][:], xt_plane[c][:], xt_bf[c])
+
+        def group_wb(h, share=S_COLS):
+            group(nc.vector.tensor_copy, wb_bf[h], wb_raw[h], share, HALF)
+            if share:
+                group(nc.scalar.copy, wb_bf[h], wb_raw[h], 0, share)
+
+        def quant_wb(h):
+            quant(wb_codes[h][:], wb_plane[h][:], wb_bf[h])
+
+        def xq_pass(out, c, z, rhs, rhs_scale, start, stop):
+            cols = slice((c % 2) * P, (c % 2 + 1) * P)
+            nc.tensor.matmul_mx(
+                out=out, lhsT=xq_codes[c // 2][:, z, cols].bitcast(FP8X4), lhsT_scale=early[:, z, tok(c)],
+                rhs=rhs, rhs_scale=rhs_scale, start=start, stop=stop,
+            )
+
+        def xt_pass(out, c, rhs, rhs_scale, start, stop):
+            nc.tensor.matmul_mx(
+                out=out, lhsT=xt_codes[c][:].bitcast(FP8X4), lhsT_scale=xt_plane[c][:],
+                rhs=rhs, rhs_scale=rhs_scale, start=start, stop=stop,
+            )
+
+        def r_xq(c, h, first):
+            for z in range(2):
+                xq_pass(r_bank(c, h)[:, half(h)], c, z, ws_codes[h][:, z, :].bitcast(FP8X4),
+                        early[4 + 4 * z :, 0, half(h)], first and z == 0, (not first) and z == 1)
+
+        def r_xt(c, h, first):
+            xt_pass(r_bank(c, h)[:, half(h)], c, wb_codes[h][:].bitcast(FP8X4), wb_plane[h][:], first, not first)
+
+        def p_xq(c):
+            for z in range(2):
+                xq_pass(p_ps[c][:], c, z, wq_codes[:, z, :].bitcast(FP4X4), late[:, 1 + z, :], z == 0, False)
+
+        def p_xt(c):
+            xt_pass(p_ps[c][:], c, wa_codes[:].bitcast(FP4X4), late[:, 0, :], False, True)
+
+        def s_abs(u):
+            nc.scalar.activation(out=mag[u][:], in_=dealt(r_bank(*u), u[1]), func=ACT.Abs)
+
+        def s_root(u):
+            nc.scalar.activation(out=root[u][:], in_=mag[u][:], func=ACT.Abs_reciprocal_sqrt, bias=1.0)
+
+        def s_square(u):
+            nc.scalar.activation(out=inv[u][:], in_=root[u][:], func=ACT.Square)
+
+        def s_unit(*us):
+            for step in (s_abs, s_root, s_square):
+                for u in us:
+                    step(u)
+
+        def v_soft(u):
+            nc.vector.tensor_tensor(out=soft[u][:], in0=dealt(r_bank(*u), u[1]), in1=inv[u][:], op=MULT)
+
+        def v_prod(u):
+            c, h = u
+            m = slice(h * HALF // PACK, (h + 1) * HALF // PACK)
+            nc.vector.tensor_tensor(out=y_tok[c][:, :, m], in0=dealt(p_ps[c], h), in1=soft[u][:], op=MULT)
+
+        turned = {}
+
+        def turn(c):
+            bank = ps.tile([P, PACK, P], F32, name="y_ps%d" % c, tag=Y_TAG[c])
+            for j in range(PACK):
+                nc.tensor.transpose(bank[:, j, :], y_tok[c][:, j, :], ident[:])
+            turned[c] = bank
+
+        def evac(c, e="ACT"):
+            copier(e)(out=y_out[c][:], in_=turned[c][:])
+
+        def store_y(c):
+            nc.sync.dma_start(out=out_rows[:, :, tok(c)], in_=y_out[c][:])
+
+        def group_y(c, e="DVE"):
+            group(copier(e), y_bf[c], y_out[c], 0, P)
+
+        def group_y_psum(c, e="DVE"):
+            copier(e)(out=y_bf[c][:], in_=turned[c][:].rearrange("p j t -> p t j"))
+
+        def g_square(u):
+            nc.gpsimd.tensor_tensor(out=inv[u][:], in0=root[u][:], in1=root[u][:], op=MULT)
+
+        def v_left(u):
+            nc.vector.tensor_tensor(out=soft[u][:], in0=dealt(r_bank(*u), u[1]), in1=root[u][:], op=MULT)
+
+        def v_right(u):
+            nc.vector.tensor_tensor(out=inv[u][:], in0=dealt(p_ps[u[0]], u[1]), in1=root[u][:], op=MULT)
+
+        def both(u, e="DVE"):
+            c, h = u
+            m = slice(h * HALF // PACK, (h + 1) * HALF // PACK)
+            eng = nc.vector if e == "DVE" else nc.gpsimd
+            eng.tensor_tensor(out=y_tok[c][:, :, m], in0=inv[u][:], in1=soft[u][:], op=MULT)
+
+        def zero_planes():
+            nc.vector.memset(early[:].bitcast(U32), 0)
+            nc.vector.memset(late[:].bitcast(U32), 0)
+
+        def warm_up():
+            nc.gpsimd.memset(warm[:], 1.0)
+            nc.scalar.activation(out=warm_out[:], in_=warm[:], func=ACT.Abs_reciprocal_sqrt, bias=1.0)
+            make_identity(nc, ident[:])
+
+        def load_xq_plane(eng):
+            load_plane(eng, early, xq_scales)
+
+        def load_wq_plane(eng):
+            load_plane(eng, late[:, 1:3, :], wq_scales)
+
+        def load_wa_plane(eng):
+            load_plane(eng, late[:, 0:1, :], wa_scales)
+
+
+        def quant_y(c):
+            quant(y_codes[:, tok(c)], y_plane[:, tok(c)], y_bf[c])
+
+        def store_codes(lo, hi):
+            dst = out_1.rearrange("z p t r -> p (z t r)").bitcast(I32)
+            nc.sync.dma_start(out=dst[:, lo * P : hi * P], in_=y_codes[:, lo * P : hi * P].bitcast(I32))
+
+        def store_plane():
+            for q in range(QUADS):
+                eng = nc.scalar if q % 2 else nc.sync
+                eng.dma_start(
+                    out=out_2[0, 4 * q : 4 * q + 4, :].bitcast(I32),
+                    in_=y_plane[32 * q : 32 * q + 4, :].bitcast(I32),
+                )
+
+
+        zero_planes()
+        load_wq_plane(nc.gpsimd)
+        warm_up()
+        load_xt(0)
+        load_xq_plane(nc.sync)
+        load_wb(0)
+        load_xq(0)
+        load_ws(0)
+        load_ws_plane(nc.sync)
+        load_xt(1)
+        load_wb(1)
+        load_ws(1)
+        load_wq()
+        load_xq(1)
+        load_xt(2)
+        load_wa()
+        load_xt(3)
+        load_wa_plane(nc.sync)
+
+        group_xt(0)
+        quant_xt(0)
+        group_wb(0)
+        quant_wb(0)
+        r_xt(0, 0, True)
+        r_xq(0, 0, False)
+        r_xq(1, 0, True)
+        group_xt(1)
+        quant_xt(1)
+        r_xt(1, 0, False)
+        s_unit((0, 0), (1, 0))
+        group_wb(1, 0)
+        quant_wb(1)
+        r_xq(0, 1, True)
+        r_xq(1, 1, True)
+        r_xt(0, 1, False)
+        r_xt(1, 1, False)
+        p_xq(0)
+        v_soft((0, 0))
+        v_soft((1, 0))
+        s_unit((0, 1), (1, 1))
+        group_xt(2)
+        quant_xt(2)
+        p_xq(1)
+        r_xq(2, 0, True)
+        r_xt(2, 0, False)
+        r_xq(2, 1, True)
+        r_xt(2, 1, False)
+        p_xt(0)
+        p_xt(1)
+        group_xt(3)
+        v_soft((0, 1))
+        quant_xt(3)
+        v_soft((1, 1))
+        s_unit((2, 0), (2, 1))
+        r_xq(3, 0, True)
+        r_xt(3, 0, False)
+        r_xq(3, 1, True)
+        r_xt(3, 1, False)
+        v_prod((0, 0))
+        v_prod((0, 1))
+        p_xq(2)
+        p_xt(2)
+        turn(0)
+        v_prod((1, 0))
+        v_prod((1, 1))
+        p_xq(3)
+        turn(1)
+        p_xt(3)
+        v_soft((2, 0))
+        v_soft((2, 1))
+        s_unit((3, 0), (3, 1))
+        v_prod((2, 0))
+        v_prod((2, 1))
+        turn(2)
+        evac(0)
+        store_y(0)
+        evac(1)
+        store_y(1)
+        v_soft((3, 0))
+        v_soft((3, 1))
+        v_prod((3, 0))
+        v_prod((3, 1))
+        turn(3)
+        group_y(0)
+        group_y(1)
+        evac(2)
+        store_y(2)
+        quant_y(0)
+        quant_y(1)
+        group_y(2)
+        evac(3)
+        store_y(3)
+        quant_y(2)
+        store_codes(0, 3)
+        group_y(3)
+        quant_y(3)
+        store_codes(3, 4)
+        store_plane()

@@ -66,10 +66,10 @@ def tile_mix_product_of_two_sums_pl_kernel(
         y_out = [new("y_out%d" % c, [P, PACK, P], F32) for c in range(TILES)]
         y_bf = [new("y_bf%d" % c, [P, P, PACK], BF16) for c in range(TILES)]
         units = [(c, h) for h in range(2) for c in range(TILES)]
-        mag = {u: new("mag%d_%d" % u, [P, PACK, HALF // PACK], F32) for u in units}
-        root = {u: new("root%d_%d" % u, [P, PACK, HALF // PACK], F32) for u in units}
-        inv = {u: new("inv%d_%d" % u, [P, PACK, HALF // PACK], F32) for u in units}
-        soft = {u: new("soft%d_%d" % u, [P, PACK, HALF // PACK], F32) for u in units}
+        mag = {u: new("mag%d_%d" % u, [P, PACK, HALF // PACK] if u[0] < 2 else [P, 2, P], F32) for u in units}
+        root = {u: new("root%d_%d" % u, [P, PACK, HALF // PACK] if u[0] < 2 else [P, 2, P], F32) for u in units}
+        inv = {u: new("inv%d_%d" % u, [P, PACK, HALF // PACK] if u[0] < 2 else [P, 2, P], F32) for u in units}
+        soft = {u: new("soft%d_%d" % u, [P, PACK, HALF // PACK] if u[0] < 2 else [P, 2, P], F32) for u in units}
         r_ps = {}
         R_TAG = {(0, 0): "a", (1, 0): "b", (0, 1): "c", (1, 1): "d", (2, 0): "a", (3, 0): "b"}
         Y_TAG = ["c", "d", "p_ps0", "p_ps1"]
@@ -89,8 +89,20 @@ def tile_mix_product_of_two_sums_pl_kernel(
         def half(h):
             return slice(h * HALF, (h + 1) * HALF)
 
-        def dealt(bank, h):
-            return bank[:, half(h)].rearrange("t (m j) -> t j m", j=PACK)
+        def dealt(bank, u):
+            c, h = u
+            if c < 2:
+                return bank[:, half(h)].rearrange("t (m j) -> t j m", j=PACK)
+            return bank[:].rearrange("t (m j) -> t j m", j=PACK)[:, 2 * h : 2 * h + 2, :]
+
+        def ushape(u):
+            return [P, PACK, HALF // PACK] if u[0] < 2 else [P, 2, P]
+
+        def y_part(u):
+            c, h = u
+            if c < 2:
+                return y_tok[c][:, :, h * HALF // PACK : (h + 1) * HALF // PACK]
+            return y_tok[c][:, 2 * h : 2 * h + 2, :]
 
         def load_xt(c):
             nc.sync.dma_start(out=xt_raw[c][:], in_=xt_rows[:, :, tok(c)])
@@ -171,6 +183,16 @@ def tile_mix_product_of_two_sums_pl_kernel(
         def r_xt(c, h, first):
             xt_pass(r_bank(c, h)[:, half(h)], c, wb_codes[h][:].bitcast(FP8X4), wb_plane[h][:], first, not first)
 
+        def r_full_xq(c):
+            for h in range(2):
+                for z in range(2):
+                    xq_pass(r_bank(c, h)[:, half(h)], c, z, ws_codes[h][:, z, :].bitcast(FP8X4),
+                            early[4 + 4 * z :, 0, half(h)], h == 0 and z == 0, False)
+
+        def r_full_xt(c):
+            for h in range(2):
+                xt_pass(r_bank(c, h)[:, half(h)], c, wb_codes[h][:].bitcast(FP8X4), wb_plane[h][:], False, h == 1)
+
         def p_xq(c):
             for z in range(2):
                 xq_pass(p_ps[c][:], c, z, wq_codes[:, z, :].bitcast(FP4X4), late[:, 1 + z, :], z == 0, False)
@@ -179,7 +201,7 @@ def tile_mix_product_of_two_sums_pl_kernel(
             xt_pass(p_ps[c][:], c, wa_codes[:].bitcast(FP4X4), late[:, 0, :], False, True)
 
         def s_abs(u):
-            nc.scalar.activation(out=mag[u][:], in_=dealt(r_bank(*u), u[1]), func=ACT.Abs)
+            nc.scalar.activation(out=mag[u][:], in_=dealt(r_bank(*u), u), func=ACT.Abs)
 
         def s_root(u):
             nc.scalar.activation(out=root[u][:], in_=mag[u][:], func=ACT.Abs_reciprocal_sqrt, bias=1.0)
@@ -193,12 +215,12 @@ def tile_mix_product_of_two_sums_pl_kernel(
                     step(u)
 
         def v_soft(u):
-            nc.vector.tensor_tensor(out=soft[u][:], in0=dealt(r_bank(*u), u[1]), in1=inv[u][:], op=MULT)
+            nc.vector.tensor_tensor(out=soft[u][:], in0=dealt(r_bank(*u), u), in1=inv[u][:], op=MULT)
 
         def v_prod(u):
             c, h = u
             m = slice(h * HALF // PACK, (h + 1) * HALF // PACK)
-            nc.vector.tensor_tensor(out=y_tok[c][:, :, m], in0=dealt(p_ps[c], h), in1=soft[u][:], op=MULT)
+            nc.vector.tensor_tensor(out=y_part(u), in0=dealt(p_ps[c], u), in1=soft[u][:], op=MULT)
 
         turned = {}
 
@@ -207,6 +229,40 @@ def tile_mix_product_of_two_sums_pl_kernel(
             for j in range(PACK):
                 nc.tensor.transpose(bank[:, j, :], y_tok[c][:, j, :], ident[:])
             turned[c] = bank
+
+        again = {}
+
+        def turn_again(c):
+            bank = ps.tile([P, PACK, P], F32, name="y_again%d" % c, tag="a")
+            for j in range(PACK):
+                nc.tensor.transpose(bank[:, j, :], y_tok[c][:, j, :], ident[:])
+            again[c] = bank
+
+        def group_again(c):
+            nc.vector.tensor_copy(out=y_bf[c][:], in_=again[c][:].rearrange("p j t -> p t j"))
+
+        def s_two(*us):
+            for step in (s_abs, s_root):
+                for u in us:
+                    step(u)
+
+        def v_square(u):
+            nc.vector.tensor_tensor(out=inv[u][:], in0=root[u][:], in1=root[u][:], op=MULT)
+
+        pair_bank = {}
+        PAIR_TAG = {(3, 0): "a", (3, 1): "p_ps1"}
+
+        def turn_pair(c, k):
+            bank = ps.tile([P, 2, P], F32, name="y_pair%d_%d" % (c, k), tag=PAIR_TAG[c, k])
+            for j in range(2):
+                nc.tensor.transpose(bank[:, j, :], y_tok[c][:, 2 * k + j, :], ident[:])
+            pair_bank[c, k] = bank
+
+        def evac_pair(c, k, e="ACT"):
+            copier(e)(out=y_out[c][:, 2 * k : 2 * k + 2, :], in_=pair_bank[c, k][:])
+
+        def store_pair(c, k):
+            nc.sync.dma_start(out=out_rows[:, 2 * k : 2 * k + 2, tok(c)], in_=y_out[c][:, 2 * k : 2 * k + 2, :])
 
         def evac(c, e="ACT"):
             copier(e)(out=y_out[c][:], in_=turned[c][:])
@@ -224,16 +280,16 @@ def tile_mix_product_of_two_sums_pl_kernel(
             nc.gpsimd.tensor_tensor(out=inv[u][:], in0=root[u][:], in1=root[u][:], op=MULT)
 
         def v_left(u):
-            nc.vector.tensor_tensor(out=soft[u][:], in0=dealt(r_bank(*u), u[1]), in1=root[u][:], op=MULT)
+            nc.vector.tensor_tensor(out=soft[u][:], in0=dealt(r_bank(*u), u), in1=root[u][:], op=MULT)
 
         def v_right(u):
-            nc.vector.tensor_tensor(out=inv[u][:], in0=dealt(p_ps[u[0]], u[1]), in1=root[u][:], op=MULT)
+            nc.vector.tensor_tensor(out=inv[u][:], in0=dealt(p_ps[u[0]], u), in1=root[u][:], op=MULT)
 
         def both(u, e="DVE"):
             c, h = u
             m = slice(h * HALF // PACK, (h + 1) * HALF // PACK)
             eng = nc.vector if e == "DVE" else nc.gpsimd
-            eng.tensor_tensor(out=y_tok[c][:, :, m], in0=inv[u][:], in1=soft[u][:], op=MULT)
+            eng.tensor_tensor(out=y_part(u), in0=inv[u][:], in1=soft[u][:], op=MULT)
 
         def zero_planes():
             nc.vector.memset(early[:].bitcast(U32), 0)
@@ -271,7 +327,6 @@ def tile_mix_product_of_two_sums_pl_kernel(
 
 
         zero_planes()
-        load_wq_plane(nc.gpsimd)
         warm_up()
         load_xt(0)
         load_xq_plane(nc.sync)
@@ -283,10 +338,11 @@ def tile_mix_product_of_two_sums_pl_kernel(
         load_wb(1)
         load_ws(1)
         load_wq()
+        load_wq_plane(nc.sync)
         load_xq(1)
         load_xt(2)
-        load_wa()
         load_xt(3)
+        load_wa()
         load_wa_plane(nc.sync)
 
         group_xt(0)
@@ -299,9 +355,10 @@ def tile_mix_product_of_two_sums_pl_kernel(
         group_xt(1)
         quant_xt(1)
         r_xt(1, 0, False)
-        s_unit((0, 0), (1, 0))
+        s_unit((0, 0))
         group_wb(1, 0)
         quant_wb(1)
+        s_unit((1, 0))
         r_xq(0, 1, True)
         r_xq(1, 1, True)
         r_xt(0, 1, False)
@@ -313,21 +370,17 @@ def tile_mix_product_of_two_sums_pl_kernel(
         group_xt(2)
         quant_xt(2)
         p_xq(1)
-        r_xq(2, 0, True)
-        r_xt(2, 0, False)
-        r_xq(2, 1, True)
-        r_xt(2, 1, False)
+        r_full_xq(2)
+        r_full_xt(2)
         p_xt(0)
-        p_xt(1)
         group_xt(3)
         v_soft((0, 1))
         quant_xt(3)
         v_soft((1, 1))
         s_unit((2, 0), (2, 1))
-        r_xq(3, 0, True)
-        r_xt(3, 0, False)
-        r_xq(3, 1, True)
-        r_xt(3, 1, False)
+        p_xt(1)
+        r_full_xq(3)
+        r_full_xt(3)
         v_prod((0, 0))
         v_prod((0, 1))
         p_xq(2)
@@ -335,36 +388,39 @@ def tile_mix_product_of_two_sums_pl_kernel(
         turn(0)
         v_prod((1, 0))
         v_prod((1, 1))
-        p_xq(3)
         turn(1)
+        p_xq(3)
         p_xt(3)
+        s_unit((3, 0), (3, 1))
         v_soft((2, 0))
         v_soft((2, 1))
-        s_unit((3, 0), (3, 1))
         v_prod((2, 0))
         v_prod((2, 1))
         turn(2)
-        evac(0)
+        evac(0, "DVE")
         store_y(0)
         evac(1)
         store_y(1)
         v_soft((3, 0))
         v_soft((3, 1))
         v_prod((3, 0))
+        turn_pair(3, 0)
         v_prod((3, 1))
-        turn(3)
-        group_y(0)
-        group_y(1)
+        turn_pair(3, 1)
         evac(2)
         store_y(2)
+        group_y(0)
+        group_y(1)
+        evac_pair(3, 0)
+        store_pair(3, 0)
         quant_y(0)
-        quant_y(1)
         group_y(2)
-        evac(3)
-        store_y(3)
-        quant_y(2)
-        store_codes(0, 3)
+        quant_y(1)
+        evac_pair(3, 1)
+        store_pair(3, 1)
+        store_codes(0, 2)
         group_y(3)
+        quant_y(2)
         quant_y(3)
-        store_codes(3, 4)
+        store_codes(2, 4)
         store_plane()

from contextlib import ExitStack

import concourse.mybir as mybir
from concourse.masks import make_identity

K, L, T, N = 512, 1024, 512, 512
FLOPS = 2 * 2 * (K + L) * T * N

F32 = mybir.dt.float32
BF16 = mybir.dt.bfloat16
I32 = mybir.dt.int32
U32 = mybir.dt.uint32
U8 = mybir.dt.uint8
FP8X4 = mybir.dt.float8_e4m3fn_x4
FP4X4 = mybir.dt.float4_e2m1fn_x4
ACT = mybir.ActivationFunctionType
MULT = mybir.AluOpType.mult

P = 128
PACK = 4
TILES = T // P
HALF = N // 2
QUADS = 4
S_COLS = 80


def tile_mix_product_of_two_sums_pl_kernel(
    tc, xt, wa_words, wa_scales, xq_words, xq_scales, wq_words, wq_scales, wb, ws_words, ws_scales,
    out_0, out_1, out_2,
):
    nc = tc.nc
    with ExitStack() as ctx:
        sb = ctx.enter_context(tc.tile_pool(name="sb", bufs=1))
        ps = ctx.enter_context(tc.psum_pool(name="ps", bufs=1))
        ctx.enter_context(tc.manual_schedule())

        def new(name, shape, dtype):
            return sb.tile(shape, dtype, name=name, align_bytes=64)

        xt_rows = xt.rearrange("(p j) t -> p j t", j=PACK)
        wb_rows = wb.rearrange("(p j) n -> p j n", j=PACK)
        out_rows = out_0.rearrange("(p j) t -> p j t", j=PACK)
        xq_src = xq_words.rearrange("z p t r -> p z (t r)").bitcast(I32)
        ws_src = ws_words.rearrange("z p n r -> p z (n r)").bitcast(I32)

        xt_raw = [new("xt_raw%d" % c, [P, PACK, P], F32) for c in range(TILES)]
        xt_bf = [new("xt_bf%d" % c, [P, P, PACK], BF16) for c in range(TILES)]
        xt_codes = [new("xt_codes%d" % c, [P, P], U32) for c in range(TILES)]
        xt_plane = [new("xt_plane%d" % c, [P, P], U8) for c in range(TILES)]
        wb_raw = [new("wb_raw%d" % h, [P, PACK, HALF], F32) for h in range(2)]
        wb_bf = [new("wb_bf%d" % h, [P, HALF, PACK], BF16) for h in range(2)]
        wb_codes = [new("wb_codes%d" % h, [P, HALF], U32) for h in range(2)]
        wb_plane = [new("wb_plane%d" % h, [P, HALF], U8) for h in range(2)]
        xq_codes = [new("xq_codes%d" % h, [P, 2, 2 * P], I32) for h in range(2)]
        ws_codes = [new("ws_codes%d" % h, [P, 2, HALF], I32) for h in range(2)]
        wa_codes = new("wa_codes", [P, 2 * N], U8)
        wq_codes = new("wq_codes", [P, 2, 2 * N], U8)
        early = new("early", [P, 2, N], U8)
        late = new("late", [P, 3, N], U8)
        ident = new("ident", [P, P], F32)
        warm = new("warm", [P, 16], F32)
        warm_out = new("warm_out", [P, 16], F32)
        y_codes = new("y_codes", [P, T], U32)
        y_plane = new("y_plane", [P, T], U8)
        y_tok = [new("y_tok%d" % c, [P, PACK, P], F32) for c in range(TILES)]
        y_out = [new("y_out%d" % c, [P, PACK, P], F32) for c in range(TILES)]
        y_bf = [new("y_bf%d" % c, [P, P, PACK], BF16) for c in range(TILES)]
        units = [(c, h) for h in range(2) for c in range(TILES)]
        mag = {u: new("mag%d_%d" % u, [P, PACK, HALF // PACK] if u[0] < 2 else [P, 2, P], F32) for u in units}
        root = {u: new("root%d_%d" % u, [P, PACK, HALF // PACK] if u[0] < 2 else [P, 2, P], F32) for u in units}
        inv = {u: new("inv%d_%d" % u, [P, PACK, HALF // PACK] if u[0] < 2 else [P, 2, P], F32) for u in units}
        soft = {u: new("soft%d_%d" % u, [P, PACK, HALF // PACK] if u[0] < 2 else [P, 2, P], F32) for u in units}
        r_ps = {}
        R_TAG = {(0, 0): "a", (1, 0): "b", (0, 1): "c", (1, 1): "d", (2, 0): "a", (3, 0): "b"}
        Y_TAG = ["c", "d", "p_ps0", "p_ps1"]

        def r_bank(c, h):
            if c >= 2:
                h = 0
            if (c, h) not in r_ps:
                r_ps[c, h] = ps.tile([P, N], F32, name="r_ps%d_%d" % (c, h), tag=R_TAG[c, h])
            return r_ps[c, h]

        p_ps = [ps.tile([P, N], F32, name="p_ps%d" % c) for c in range(TILES)]

        def tok(c):
            return slice(c * P, (c + 1) * P)

        def half(h):
            return slice(h * HALF, (h + 1) * HALF)

        def dealt(bank, u):
            c, h = u
            if c < 2:
                return bank[:, half(h)].rearrange("t (m j) -> t j m", j=PACK)
            return bank[:].rearrange("t (m j) -> t j m", j=PACK)[:, 2 * h : 2 * h + 2, :]

        def ushape(u):
            return [P, PACK, HALF // PACK] if u[0] < 2 else [P, 2, P]

        def y_part(u):
            c, h = u
            if c < 2:
                return y_tok[c][:, :, h * HALF // PACK : (h + 1) * HALF // PACK]
            return y_tok[c][:, 2 * h : 2 * h + 2, :]

        def load_xt(c):
            nc.sync.dma_start(out=xt_raw[c][:], in_=xt_rows[:, :, tok(c)])

        def load_wb(h):
            nc.sync.dma_start(out=wb_raw[h][:], in_=wb_rows[:, :, half(h)])

        def load_xq(h):
            nc.sync.dma_start(out=xq_codes[h][:], in_=xq_src[:, :, half(h)])

        def load_ws(h):
            nc.sync.dma_start(out=ws_codes[h][:], in_=ws_src[:, :, half(h)])

        def load_wa():
            nc.sync.dma_start(out=wa_codes[:].bitcast(I32), in_=wa_words[0].bitcast(I32))

        def load_wq():
            nc.sync.dma_start(out=wq_codes[:].bitcast(I32), in_=wq_words.rearrange("z p b -> p z b").bitcast(I32))

        def load_plane(eng, dst, src):
            for q in range(QUADS):
                eng.dma_start(
                    out=dst[32 * q : 32 * q + 4].bitcast(I32),
                    in_=src[:, 4 * q : 4 * q + 4, :].rearrange("z r c -> r z c").bitcast(I32),
                )

        def load_ws_plane(eng):
            for q in range(QUADS):
                eng.dma_start(
                    out=early[32 * q + 4 : 32 * q + 12, 0, :].bitcast(I32),
                    in_=ws_scales[:, 4 * q : 4 * q + 4, :].bitcast(I32),
                )

        def group(copy, dst, src, lo, hi):
            copy(
                out=dst[:, lo:hi, :].rearrange("p (c i) j -> p c j i", i=4),
                in_=src[:, :, lo:hi].rearrange("p j (c i) -> p c j i", i=4),
            )

        def quant(codes, plane, src):
            nc.vector.quantize_mx(out=codes.bitcast(FP8X4), scales=plane, in_=src[:].rearrange("p c j -> p (c j)"))

        def copier(e):
            return {"DVE": nc.vector.tensor_copy, "ACT": nc.scalar.copy, "POOL": nc.gpsimd.tensor_copy}[e]

        def group_xt(c, e="DVE"):
            group(copier(e), xt_bf[c], xt_raw[c], 0, P)

        def quant_xt(c):
            quant(xt_codes[c][:], xt_plane[c][:], xt_bf[c])

        def group_wb(h, share=S_COLS):
            group(nc.vector.tensor_copy, wb_bf[h], wb_raw[h], share, HALF)
            if share:
                group(nc.scalar.copy, wb_bf[h], wb_raw[h], 0, share)

        def quant_wb(h):
            quant(wb_codes[h][:], wb_plane[h][:], wb_bf[h])

        def xq_pass(out, c, z, rhs, rhs_scale, start, stop):
            cols = slice((c % 2) * P, (c % 2 + 1) * P)
            nc.tensor.matmul_mx(
                out=out, lhsT=xq_codes[c // 2][:, z, cols].bitcast(FP8X4), lhsT_scale=early[:, z, tok(c)],
                rhs=rhs, rhs_scale=rhs_scale, start=start, stop=stop,
            )

        def xt_pass(out, c, rhs, rhs_scale, start, stop):
            nc.tensor.matmul_mx(
                out=out, lhsT=xt_codes[c][:].bitcast(FP8X4), lhsT_scale=xt_plane[c][:],
                rhs=rhs, rhs_scale=rhs_scale, start=start, stop=stop,
            )

        def r_xq(c, h, first):
            for z in range(2):
                xq_pass(r_bank(c, h)[:, half(h)], c, z, ws_codes[h][:, z, :].bitcast(FP8X4),
                        early[4 + 4 * z :, 0, half(h)], first and z == 0, (not first) and z == 1)

        def r_xt(c, h, first):
            xt_pass(r_bank(c, h)[:, half(h)], c, wb_codes[h][:].bitcast(FP8X4), wb_plane[h][:], first, not first)

        def r_full_xq(c):
            for h in range(2):
                for z in range(2):
                    xq_pass(r_bank(c, h)[:, half(h)], c, z, ws_codes[h][:, z, :].bitcast(FP8X4),
                            early[4 + 4 * z :, 0, half(h)], h == 0 and z == 0, False)

        def r_full_xt(c):
            for h in range(2):
                xt_pass(r_bank(c, h)[:, half(h)], c, wb_codes[h][:].bitcast(FP8X4), wb_plane[h][:], False, h == 1)

        def p_xq(c):
            for z in range(2):
                xq_pass(p_ps[c][:], c, z, wq_codes[:, z, :].bitcast(FP4X4), late[:, 1 + z, :], z == 0, False)

        def p_xt(c):
            xt_pass(p_ps[c][:], c, wa_codes[:].bitcast(FP4X4), late[:, 0, :], False, True)

        def s_abs(u):
            nc.scalar.activation(out=mag[u][:], in_=dealt(r_bank(*u), u), func=ACT.Abs)

        def s_root(u):
            nc.scalar.activation(out=root[u][:], in_=mag[u][:], func=ACT.Abs_reciprocal_sqrt, bias=1.0)

        def s_square(u):
            nc.scalar.activation(out=inv[u][:], in_=root[u][:], func=ACT.Square)

        def s_unit(*us):
            for step in (s_abs, s_root, s_square):
                for u in us:
                    step(u)

        def v_soft(u):
            nc.vector.tensor_tensor(out=soft[u][:], in0=dealt(r_bank(*u), u), in1=inv[u][:], op=MULT)

        def v_prod(u):
            c, h = u
            m = slice(h * HALF // PACK, (h + 1) * HALF // PACK)
            nc.vector.tensor_tensor(out=y_part(u), in0=dealt(p_ps[c], u), in1=soft[u][:], op=MULT)

        turned = {}

        def turn(c):
            bank = ps.tile([P, PACK, P], F32, name="y_ps%d" % c, tag=Y_TAG[c])
            for j in range(PACK):
                nc.tensor.transpose(bank[:, j, :], y_tok[c][:, j, :], ident[:])
            turned[c] = bank

        again = {}

        def turn_again(c):
            bank = ps.tile([P, PACK, P], F32, name="y_again%d" % c, tag="a")
            for j in range(PACK):
                nc.tensor.transpose(bank[:, j, :], y_tok[c][:, j, :], ident[:])
            again[c] = bank

        def group_again(c):
            nc.vector.tensor_copy(out=y_bf[c][:], in_=again[c][:].rearrange("p j t -> p t j"))

        def s_two(*us):
            for step in (s_abs, s_root):
                for u in us:
                    step(u)

        def v_square(u):
            nc.vector.tensor_tensor(out=inv[u][:], in0=root[u][:], in1=root[u][:], op=MULT)

        pair_bank = {}
        PAIR_TAG = {(3, 0): "a", (3, 1): "p_ps1"}

        def turn_pair(c, k):
            bank = ps.tile([P, 2, P], F32, name="y_pair%d_%d" % (c, k), tag=PAIR_TAG[c, k])
            for j in range(2):
                nc.tensor.transpose(bank[:, j, :], y_tok[c][:, 2 * k + j, :], ident[:])
            pair_bank[c, k] = bank

        def evac_pair(c, k, e="ACT"):
            copier(e)(out=y_out[c][:, 2 * k : 2 * k + 2, :], in_=pair_bank[c, k][:])

        def store_pair(c, k):
            nc.sync.dma_start(out=out_rows[:, 2 * k : 2 * k + 2, tok(c)], in_=y_out[c][:, 2 * k : 2 * k + 2, :])

        def evac(c, e="ACT"):
            copier(e)(out=y_out[c][:], in_=turned[c][:])

        def store_y(c):
            nc.sync.dma_start(out=out_rows[:, :, tok(c)], in_=y_out[c][:])

        def group_y(c, e="DVE"):
            group(copier(e), y_bf[c], y_out[c], 0, P)

        def group_y_psum(c, e="DVE"):
            copier(e)(out=y_bf[c][:], in_=turned[c][:].rearrange("p j t -> p t j"))

        def g_square(u):
            nc.gpsimd.tensor_tensor(out=inv[u][:], in0=root[u][:], in1=root[u][:], op=MULT)

        def v_left(u):
            nc.vector.tensor_tensor(out=soft[u][:], in0=dealt(r_bank(*u), u), in1=root[u][:], op=MULT)

        def v_right(u):
            nc.vector.tensor_tensor(out=inv[u][:], in0=dealt(p_ps[u[0]], u), in1=root[u][:], op=MULT)

        def both(u, e="DVE"):
            c, h = u
            m = slice(h * HALF // PACK, (h + 1) * HALF // PACK)
            eng = nc.vector if e == "DVE" else nc.gpsimd
            eng.tensor_tensor(out=y_part(u), in0=inv[u][:], in1=soft[u][:], op=MULT)

        def zero_planes():
            nc.vector.memset(early[:].bitcast(U32), 0)
            nc.vector.memset(late[:].bitcast(U32), 0)

        def warm_up():
            nc.gpsimd.memset(warm[:], 1.0)
            nc.scalar.activation(out=warm_out[:], in_=warm[:], func=ACT.Abs_reciprocal_sqrt, bias=1.0)
            make_identity(nc, ident[:])

        def load_xq_plane(eng):
            load_plane(eng, early, xq_scales)

        def load_wq_plane(eng):
            load_plane(eng, late[:, 1:3, :], wq_scales)

        def load_wa_plane(eng):
            load_plane(eng, late[:, 0:1, :], wa_scales)


        def quant_y(c):
            quant(y_codes[:, tok(c)], y_plane[:, tok(c)], y_bf[c])

        def store_codes(lo, hi):
            dst = out_1.rearrange("z p t r -> p (z t r)").bitcast(I32)
            nc.sync.dma_start(out=dst[:, lo * P : hi * P], in_=y_codes[:, lo * P : hi * P].bitcast(I32))

        def store_plane():
            for q in range(QUADS):
                eng = nc.scalar if q % 2 else nc.sync
                eng.dma_start(
                    out=out_2[0, 4 * q : 4 * q + 4, :].bitcast(I32),
                    in_=y_plane[32 * q : 32 * q + 4, :].bitcast(I32),
                )


        zero_planes()
        warm_up()
        load_xt(0)
        load_xq_plane(nc.sync)
        load_wb(0)
        load_xq(0)
        load_ws(0)
        load_ws_plane(nc.sync)
        load_xt(1)
        load_wb(1)
        load_ws(1)
        load_wq()
        load_wq_plane(nc.sync)
        load_xq(1)
        load_xt(2)
        load_xt(3)
        load_wa()
        load_wa_plane(nc.sync)

        group_xt(0)
        quant_xt(0)
        group_wb(0)
        quant_wb(0)
        r_xt(0, 0, True)
        r_xq(0, 0, False)
        r_xq(1, 0, True)
        group_xt(1)
        quant_xt(1)
        r_xt(1, 0, False)
        s_unit((0, 0))
        group_wb(1, 0)
        quant_wb(1)
        s_unit((1, 0))
        r_xq(0, 1, True)
        r_xq(1, 1, True)
        r_xt(0, 1, False)
        r_xt(1, 1, False)
        p_xq(0)
        v_soft((0, 0))
        v_soft((1, 0))
        s_unit((0, 1), (1, 1))
        group_xt(2)
        quant_xt(2)
        p_xq(1)
        r_full_xq(2)
        r_full_xt(2)
        p_xt(0)
        group_xt(3)
        v_soft((0, 1))
        quant_xt(3)
        v_soft((1, 1))
        s_unit((2, 0), (2, 1))
        p_xt(1)
        r_full_xq(3)
        r_full_xt(3)
        v_prod((0, 0))
        v_prod((0, 1))
        p_xq(2)
        p_xt(2)
        turn(0)
        v_prod((1, 0))
        v_prod((1, 1))
        turn(1)
        p_xq(3)
        p_xt(3)
        s_unit((3, 0), (3, 1))
        v_soft((2, 0))
        v_soft((2, 1))
        v_prod((2, 0))
        v_prod((2, 1))
        turn(2)
        evac(0, "DVE")
        store_y(0)
        evac(1)
        store_y(1)
        v_soft((3, 0))
        v_soft((3, 1))
        v_prod((3, 0))
        turn_pair(3, 0)
        v_prod((3, 1))
        turn_pair(3, 1)
        evac(2)
        store_y(2)
        group_y(0)
        group_y(1)
        evac_pair(3, 0)
        store_pair(3, 0)
        quant_y(0)
        group_y(2)
        quant_y(1)
        evac_pair(3, 1)
        store_pair(3, 1)
        store_codes(0, 2)
        group_y(3)
        quant_y(2)
        quant_y(3)
        store_codes(2, 4)
        store_plane()
